import numpy as np
import ml_dtypes


def mxq(x, axis, fmt="e4m3"):
    dtype, down = {"e4m3": (ml_dtypes.float8_e4m3fn, 7), "e5m2": (ml_dtypes.float8_e5m2, 14)}[fmt]
    v = np.moveaxis(np.asarray(x, np.float32).astype(ml_dtypes.bfloat16).astype(np.float64), axis, -1)
    blocks = v.reshape(v.shape[:-1] + (-1, 32))
    amax = np.abs(blocks).max(-1, keepdims=True)
    byte = np.maximum(np.where(amax > 0, np.frexp(amax)[1] - 1 + 127, 0) - down, 1)
    scale = np.exp2(byte - 127.0)
    codes = (blocks / scale).astype(np.float32).astype(dtype).astype(np.float64)
    return np.moveaxis((codes * scale).reshape(v.shape), -1, axis)


WIDE = False


def mx_kscale(k):
    if not WIDE:
        return np.ones(k)
    levels = np.array([10, -10, 5, -5, 0])
    if k % 512:
        return np.exp2(np.random.permutation(np.resize(levels, k // 32))).repeat(32)
    a = np.empty((k // 512, 16))
    for p in range(k // 512):
        a[p, :8] = np.random.permutation(np.resize(levels, 8))
        for g in range(8):
            far = levels[np.abs(levels - a[p, g]) >= 10]
            a[p, g + 8] = far[np.random.randint(len(far))]
    return np.exp2(a.ravel()).repeat(32)


def f64(x):
    return np.asarray(x).astype(np.float64)


def striped(idx):
    return np.tile(idx.reshape(-1, 16).T, (8, 1)).astype(np.uint16)


def unstriped(offs):
    return offs[:16].T.reshape(-1).astype(np.int64)


def pack_weight(w):
    k, n = w.shape
    w = f64(np.asarray(w, np.float32).astype(ml_dtypes.bfloat16)).reshape(k // 32, 32, n)
    amax = np.abs(w).max(1)
    byte = np.clip(np.where(amax > 0, np.frexp(amax)[1] - 1 + 127 - 7, 1), 1, 254)
    scaled = (w * np.exp2(127.0 - byte)[:, None, :]).reshape(k, n).astype(np.float32)
    words = np.ascontiguousarray(scaled.reshape(k // 512, 128, 4, n).transpose(0, 1, 3, 2)).astype(ml_dtypes.float8_e4m3fn).view(np.uint8)
    return words, np.ascontiguousarray(byte.astype(np.uint8).reshape(k // 512, 16, n))


def unpack_weight(words, scales):
    g, p, n, _ = words.shape
    vals = np.ascontiguousarray(words).view(ml_dtypes.float8_e4m3fn).astype(np.float64) * np.repeat(np.exp2(scales.astype(np.float64) - 127.0), 8, axis=1)[..., None]
    return vals.transpose(0, 1, 3, 2).reshape(g * 512, n)


K, T, S, N, H = 1024, 2048, 512, 256, 512


def setup_inputs():
    n = np.random.standard_normal
    s = mx_kscale(K)[:, None]
    u = mx_kscale(H)
    packed_xT = pack_weight(n((K, T)) * s)
    return {
        "x_words": packed_xT[0],
        "x_scales": packed_xT[1],
        "w1": (n((K, H)) / np.sqrt(K) / s).astype(np.float32),
        "w2": (n((K, H)) / np.sqrt(K) / s).astype(np.float32),
        "ell": (0.4 * n((H, S))).astype(np.float32),
        "flx": (np.random.uniform(0.5, 1.5, (H, S))).astype(np.float32),
        "unit": (np.random.uniform(0.6, 1.4, (H, 1)) * u[:, None]).astype(np.float32),
        "w3": (n((H, N)) / np.sqrt(H) / u[:, None]).astype(np.float32),
        "offs": striped(np.random.permutation(T)[:S]),
        "src": striped(np.random.permutation(S)),
    }


def reference(x_words, x_scales, w1, w2, ell, flx, unit, w3, offs, src):
    xq = unpack_weight(x_words, x_scales)[:, unstriped(offs)]
    sh = mxq(f64(w2), 0, "e4m3").T @ xq
    shear = 0.3 * np.tanh(sh)
    kp = mxq(f64(w1), 0, "e4m3").T @ xq
    kappa = 0.4 * np.tanh(kp)
    red = shear / (-1.0 * kappa + 1.0)
    obs = (f64(ell) + red) / (red * f64(ell)[:, unstriped(src)] + 1.0)
    magn = f64(flx) / ((-1.0 * kappa + 1.0) ** 2 - ((shear) ** 2) + 0.2)
    hid = f64(unit) * (obs * magn)
    return mxq(f64(w3), 0, "e4m3").T @ mxq(hid, 0, "e4m3")

@@ -1,0 +1,220 @@
+import math
+from contextlib import ExitStack
+
+import concourse.mybir as mybir
+
+K, T, S, N, H = 1024, 2048, 512, 256, 512
+FLOPS = 2 * (2 * K * H * S + H * N * S)
+
+F32 = mybir.dt.float32
+BF16 = mybir.dt.bfloat16
+I32 = mybir.dt.int32
+U32 = mybir.dt.uint32
+U16 = mybir.dt.uint16
+U8 = mybir.dt.uint8
+FP8X4 = mybir.dt.float8_e4m3fn_x4
+ACT = mybir.ActivationFunctionType
+ALU = mybir.AluOpType
+
+P = 128
+PACK = 4
+PASSES = K // (P * PACK)
+BANK_COLS = 128
+CHUNKS = [(0, 256), (256, 256)]
+LAST_CHUNKS = [(0, 256), (256, 128), (384, 128)]
+
+
+def tile_picked_ylensg_fe_p_kernel(
+    tc, x_words, x_scales, w1, w2, ell, flx, unit, w3, offs, src, out
+):
+    nc = tc.nc
+    with ExitStack() as ctx:
+        keep = ctx.enter_context(tc.tile_pool(name="keep", bufs=1))
+        psum = ctx.enter_context(tc.psum_pool(name="psum", bufs=1))
+
+        def sb(name, shape, dtype):
+            return keep.tile(shape, dtype, name=name, align_bytes=64)
+
+        offs_sb = keep.tile([P, S // 16], U16, name="offs_sb")
+        src_sb = keep.tile([P, S // 16], U16, name="src_sb")
+        x_table = [sb(f"x_table{o}", [P, T], I32) for o in range(PASSES)]
+        scale_table = sb("scale_table", [P, T], U8)
+        x_codes = [sb(f"x_codes{o}", [P, S], U32) for o in range(PASSES)]
+        x_planes = sb("x_planes", [P, S], U8)
+
+        def load_x(o):
+            nc.sync.dma_start(x_table[o][:], x_words[o].rearrange("p n t -> p (n t)").bitcast(I32))
+
+        def gather_x(o, j0, w):
+            picked = x_table[o][:].bitcast(U32).indirect(offs_sb[:, j0 // 16 : (j0 + w) // 16])
+            nc.vector.tensor_copy(x_codes[o][:, j0 : j0 + w], picked)
+
+        def load_w(name, w, o, pieces):
+            raws = []
+            width = H // pieces
+            for h in range(pieces):
+                raw = sb(f"{name}_raw{o}_{h}", [P, PACK, width], F32)
+                rows = w[o * P * PACK : (o + 1) * P * PACK, h * width : (h + 1) * width]
+                nc.sync.dma_start(raw[:], rows.rearrange("(p j) c -> p j c", j=PACK))
+                raws.append(raw)
+            return raws
+
+        def quantise_w(name, raws, o):
+            grouped = sb(f"{name}_grouped{o}", [P, PACK * H], BF16)
+            view = grouped[:].rearrange("p (t m j) -> p m j t", t=PACK, j=PACK)
+            span = P // len(raws)
+            for h, raw in enumerate(raws):
+                nc.vector.tensor_copy(
+                    view[:, h * span : (h + 1) * span, :, :],
+                    raw[:].rearrange("p j (m t) -> p m j t", t=PACK),
+                )
+            codes = sb(f"{name}_codes{o}", [P, H], U32)
+            planes = sb(f"{name}_planes{o}", [P, H], U8)
+            nc.vector.quantize_mx(out=codes[:].bitcast(FP8X4), scales=planes[:], in_=grouped[:])
+            return codes, planes
+
+        nc.gpsimd.memset(scale_table[:].bitcast(I32), 0)
+        nc.sync.dma_start(offs_sb[:], offs)
+        load_x(0)
+        for q in range(4):
+            nc.sync.dma_start(
+                scale_table[32 * q : 32 * q + 4 * PASSES, :].bitcast(I32),
+                x_scales[:, 4 * q : 4 * q + 4, :].bitcast(I32),
+            )
+        w1_raw = [load_w("w1", w1, 0, 1), load_w("w1", w1, 1, 1)]
+        load_x(1)
+        w2_raw = [load_w("w2", w2, 0, 1), load_w("w2", w2, 1, 2)]
+        nc.sync.dma_start(src_sb[:], src)
+        ell_sb = sb("ell_sb", [P, PACK, S], F32)
+        nc.sync.dma_start(ell_sb[:], ell.rearrange("(p t) c -> p t c", t=PACK))
+        unit_sb = sb("unit_sb", [P, PACK], F32)
+        nc.sync.dma_start(unit_sb[:], unit.rearrange("(p t) o -> p (t o)", t=PACK))
+        flx_sb = sb("flx_sb", [P, PACK, S], F32)
+        nc.sync.dma_start(flx_sb[:], flx.rearrange("(p t) c -> p t c", t=PACK))
+        w3_raw = sb("w3_raw", [P, PACK, N], F32)
+        nc.sync.dma_start(w3_raw[:], w3.rearrange("(p j) c -> p j c", j=PACK))
+
+        gather_x(0, 0, S)
+        nc.vector.tensor_copy(x_planes[:], scale_table[:].indirect(offs_sb[:]))
+        w1_q = [quantise_w("w1", w1_raw[o], o) for o in range(PASSES)]
+        for j0, w in CHUNKS:
+            gather_x(1, j0, w)
+
+        def product(bank, wq, t, o, cols, start, stop):
+            codes, planes = wq[o]
+            m_cols = slice(t * P, (t + 1) * P)
+            nc.tensor.matmul_mx(
+                out=bank,
+                lhsT=codes[:, m_cols].bitcast(FP8X4),
+                lhsT_scale=planes[:, m_cols],
+                rhs=x_codes[o][:, cols].bitcast(FP8X4),
+                rhs_scale=x_planes[4 * o :, cols],
+                start=start,
+                stop=stop,
+            )
+
+        def chunk_tiles(name):
+            return [sb(f"{name}{c}", [P, PACK, w], F32) for c, (j0, w) in enumerate(CHUNKS)]
+
+        sig, tk, ts, g_sq, red, num = (chunk_tiles(n) for n in ("sig", "tk", "ts", "g_sq", "red", "num"))
+        paired, pair, den2, den, sgn, root = (chunk_tiles(n) for n in ("paired", "pair", "den2", "den", "sgn", "root"))
+        a_sq, inv, flux, signed = tk, root, num, num
+
+        kp_banks = {}
+        for c, (j0, w) in enumerate(CHUNKS):
+            for u in range(2):
+                kp_banks[c, u] = psum.tile([P, 2, w], F32, name=f"kp{c}{u}", tag=f"left{2 * c + u}")
+        for o in range(PASSES):
+            for c, (j0, w) in enumerate(CHUNKS):
+                for t in range(PACK):
+                    product(
+                        kp_banks[c, t // 2][:, t % 2, :], w1_q, t, o, slice(j0, j0 + w),
+                        o == 0 and t % 2 == 0, o == PASSES - 1 and t % 2 == 1,
+                    )
+        for c in range(len(CHUNKS)):
+            for u in range(2):
+                nc.scalar.activation(
+                    sig[c][:, 2 * u : 2 * u + 2, :], kp_banks[c, u][:], ACT.Sigmoid, bias=-math.log(7.0 / 3.0), scale=2.0
+                )
+        for c in range(len(CHUNKS)):
+            for u in range(2):
+                nc.scalar.activation(tk[c][:, 2 * u : 2 * u + 2, :], kp_banks[c, u][:], ACT.Tanh)
+
+        w2_q = [quantise_w("w2", w2_raw[o], o) for o in range(PASSES)]
+        n_banks = S // BANK_COLS
+        sh_banks = [psum.tile([P, PACK, BANK_COLS], F32, name=f"sh{b}", tag=f"right{b}") for b in range(n_banks)]
+        for o in range(PASSES):
+            for b in range(n_banks):
+                for t in range(PACK):
+                    product(
+                        sh_banks[b][:, t, :], w2_q, t, o, slice(b * BANK_COLS, (b + 1) * BANK_COLS),
+                        o == 0 and t == 0, o == PASSES - 1 and t == PACK - 1,
+                    )
+
+        for c, (j0, w) in enumerate(CHUNKS):
+            for b in range(j0 // BANK_COLS, (j0 + w) // BANK_COLS):
+                part = slice(b * BANK_COLS - j0, (b + 1) * BANK_COLS - j0)
+                nc.scalar.activation(ts[c][:, :, part], sh_banks[b][:], ACT.Tanh)
+            nc.vector.scalar_tensor_tensor(red[c][:], sig[c][:], 0.75, ts[c][:], ALU.add, ALU.mult)
+        for c, (j0, w) in enumerate(CHUNKS):
+            cols = slice(j0, j0 + w)
+            for t in range(PACK):
+                nc.scalar.activation(
+                    paired[c][:, t, :], ell_sb[:, t, :].indirect(src_sb[:, j0 // 16 : (j0 + w) // 16]), ACT.Copy
+                )
+            nc.vector.scalar_tensor_tensor(num[c][:], red[c][:], 2.0 / 7.0, ell_sb[:, :, cols], ALU.mult, ALU.add)
+        for c, (j0, w) in enumerate(CHUNKS):
+            cols = slice(j0, j0 + w)
+            nc.vector.scalar_tensor_tensor(pair[c][:], red[c][:], 2.0 / 7.0, paired[c][:], ALU.mult, ALU.mult)
+            for t in range(PACK):
+                nc.vector.scalar_tensor_tensor(
+                    flux[c][:, t, :], num[c][:, t, :], unit_sb[:, t : t + 1], flx_sb[:, t, cols], ALU.mult, ALU.mult
+                )
+        for c, (j0, w) in enumerate(CHUNKS):
+            nc.scalar.activation(a_sq[c][:], tk[c][:], ACT.Square, bias=1.0, scale=-0.4)
+            nc.scalar.activation(g_sq[c][:], ts[c][:], ACT.Square, scale=0.3)
+            nc.vector.scalar_tensor_tensor(den2[c][:], a_sq[c][:], 0.2, g_sq[c][:], ALU.add, ALU.subtract)
+            nc.vector.scalar_tensor_tensor(den[c][:], pair[c][:], 1.0, den2[c][:], ALU.add, ALU.mult)
+        for c, (j0, w) in enumerate(CHUNKS):
+            nc.scalar.activation(sgn[c][:], pair[c][:], ACT.Sign, bias=1.0)
+            nc.vector.tensor_tensor(signed[c][:], flux[c][:], sgn[c][:], ALU.mult)
+
+        w3_grouped = sb("w3_grouped", [P, N * PACK], BF16)
+        w3_codes = sb("w3_codes", [P, N], U32)
+        w3_planes = sb("w3_planes", [P, N], U8)
+        nc.vector.tensor_copy(
+            w3_grouped[:].rearrange("p (c i j) -> p c j i", i=4, j=PACK),
+            w3_raw[:].rearrange("p j (c i) -> p c j i", i=4),
+        )
+        nc.vector.quantize_mx(out=w3_codes[:].bitcast(FP8X4), scales=w3_planes[:], in_=w3_grouped[:])
+
+        for f, (j0, w) in enumerate(LAST_CHUNKS):
+            c = j0 // CHUNKS[0][1]
+            part = slice(j0 - CHUNKS[c][0], j0 - CHUNKS[c][0] + w)
+            nc.scalar.activation(root[c][:, :, part], den[c][:, :, part], ACT.Abs_reciprocal_sqrt)
+            nc.scalar.activation(inv[c][:, :, part], root[c][:, :, part], ACT.Square)
+            hid = sb(f"hid{f}", [P, w * PACK], BF16)
+            nc.vector.tensor_tensor(
+                hid[:].rearrange("p (c i t) -> p c t i", i=4, t=PACK),
+                signed[c][:, :, part].rearrange("p t (c i) -> p c t i", i=4),
+                inv[c][:, :, part].rearrange("p t (c i) -> p c t i", i=4),
+                ALU.mult,
+            )
+            hid_codes = sb(f"hid_codes{f}", [P, w], U32)
+            hid_planes = sb(f"hid_planes{f}", [P, w], U8)
+            nc.vector.quantize_mx(out=hid_codes[:].bitcast(FP8X4), scales=hid_planes[:], in_=hid[:])
+            bins = psum.tile([P, N // P, w], F32, name=f"bins{f}", tag=f"left{f}")
+            for mt in range(N // P):
+                m_cols = slice(mt * P, (mt + 1) * P)
+                nc.tensor.matmul_mx(
+                    out=bins[:, mt, :],
+                    lhsT=w3_codes[:, m_cols].bitcast(FP8X4),
+                    lhsT_scale=w3_planes[:, m_cols],
+                    rhs=hid_codes[:].bitcast(FP8X4),
+                    rhs_scale=hid_planes[:],
+                    start=True,
+                    stop=True,
+                )
+            result = sb(f"result{f}", [P, N // P, w], F32)
+            nc.scalar.copy(result[:], bins[:])
+            nc.sync.dma_start(out[:, j0 : j0 + w].rearrange("(m p) c -> p m c", p=P), result[:])

@@ -61,19 +61,19 @@ def tile_picked_ylensg_fe_p_kernel(
 
         def quantise_w(name, raws, o):
             grouped = sb(f"{name}_grouped{o}", [P, PACK * H], BF16)
-            view = grouped[:].rearrange("p (t m j) -> p m j t", t=PACK, j=PACK)
-            span = P // len(raws)
+            view = grouped[:].rearrange("p (t a i j) -> p a t j i", t=PACK, i=4, j=PACK)
+            span = P // 4 // len(raws)
             for h, raw in enumerate(raws):
                 nc.vector.tensor_copy(
-                    view[:, h * span : (h + 1) * span, :, :],
-                    raw[:].rearrange("p j (m t) -> p m j t", t=PACK),
+                    view[:, h * span : (h + 1) * span, :, :, :],
+                    raw[:].rearrange("p j (a t i) -> p a t j i", t=PACK, i=4),
                 )
             codes = sb(f"{name}_codes{o}", [P, H], U32)
             planes = sb(f"{name}_planes{o}", [P, H], U8)
             nc.vector.quantize_mx(out=codes[:].bitcast(FP8X4), scales=planes[:], in_=grouped[:])
             return codes, planes
 
-        nc.gpsimd.memset(scale_table[:].bitcast(I32), 0)
+        nc.vector.memset(scale_table[:].bitcast(I32), 0)
         nc.sync.dma_start(offs_sb[:], offs)
         load_x(0)
         for q in range(4):
@@ -85,14 +85,19 @@ def tile_picked_ylensg_fe_p_kernel(
         load_x(1)
         w2_raw = [load_w("w2", w2, 0, 1), load_w("w2", w2, 1, 2)]
         nc.sync.dma_start(src_sb[:], src)
-        ell_sb = sb("ell_sb", [P, PACK, S], F32)
-        nc.sync.dma_start(ell_sb[:], ell.rearrange("(p t) c -> p t c", t=PACK))
-        unit_sb = sb("unit_sb", [P, PACK], F32)
-        nc.sync.dma_start(unit_sb[:], unit.rearrange("(p t) o -> p (t o)", t=PACK))
-        flx_sb = sb("flx_sb", [P, PACK, S], F32)
-        nc.sync.dma_start(flx_sb[:], flx.rearrange("(p t) c -> p t c", t=PACK))
-        w3_raw = sb("w3_raw", [P, PACK, N], F32)
-        nc.sync.dma_start(w3_raw[:], w3.rearrange("(p j) c -> p j c", j=PACK))
+
+        def load_rows(queue, name, rows):
+            tile = sb(name, [P, PACK, rows.shape[1]], F32)
+            dealt = rows.rearrange("(a t i) c -> i a t c", t=PACK, i=4)
+            for i in range(4):
+                queue.dma_start(tile[i:P:4, :, :], dealt[i])
+            return tile
+
+        w3_raw = load_rows(nc.sync, "w3_raw", w3)
+        ell_sb = load_rows(nc.sync, "ell_sb", ell)
+        with nc.allow_non_contiguous_dma(reason="one value for each row"):
+            unit_sb = load_rows(nc.sync, "unit_sb", unit)
+        flx_sb = load_rows(nc.sync, "flx_sb", flx)
 
         gather_x(0, 0, S)
         nc.vector.tensor_copy(x_planes[:], scale_table[:].indirect(offs_sb[:]))
@@ -151,6 +156,15 @@ def tile_picked_ylensg_fe_p_kernel(
                         o == 0 and t == 0, o == PASSES - 1 and t == PACK - 1,
                     )
 
+        w3_grouped = sb("w3_grouped", [P, N * PACK], BF16)
+        w3_codes = sb("w3_codes", [P, N], U32)
+        w3_planes = sb("w3_planes", [P, N], U8)
+        nc.vector.tensor_copy(
+            w3_grouped[:].rearrange("p (c i j) -> p c j i", i=4, j=PACK),
+            w3_raw[:].rearrange("p j (c i) -> p c j i", i=4),
+        )
+        nc.vector.quantize_mx(out=w3_codes[:].bitcast(FP8X4), scales=w3_planes[:], in_=w3_grouped[:])
+
         for c, (j0, w) in enumerate(CHUNKS):
             for b in range(j0 // BANK_COLS, (j0 + w) // BANK_COLS):
                 part = slice(b * BANK_COLS - j0, (b + 1) * BANK_COLS - j0)
@@ -168,7 +182,7 @@ def tile_picked_ylensg_fe_p_kernel(
             nc.vector.scalar_tensor_tensor(pair[c][:], red[c][:], 2.0 / 7.0, paired[c][:], ALU.mult, ALU.mult)
             for t in range(PACK):
                 nc.vector.scalar_tensor_tensor(
-                    flux[c][:, t, :], num[c][:, t, :], unit_sb[:, t : t + 1], flx_sb[:, t, cols], ALU.mult, ALU.mult
+                    flux[c][:, t, :], num[c][:, t, :], unit_sb[:, t, :], flx_sb[:, t, cols], ALU.mult, ALU.mult
                 )
         for c, (j0, w) in enumerate(CHUNKS):
             nc.scalar.activation(a_sq[c][:], tk[c][:], ACT.Square, bias=1.0, scale=-0.4)
@@ -178,15 +192,6 @@ def tile_picked_ylensg_fe_p_kernel(
         for c, (j0, w) in enumerate(CHUNKS):
             nc.scalar.activation(sgn[c][:], pair[c][:], ACT.Sign, bias=1.0)
             nc.vector.tensor_tensor(signed[c][:], flux[c][:], sgn[c][:], ALU.mult)
-
-        w3_grouped = sb("w3_grouped", [P, N * PACK], BF16)
-        w3_codes = sb("w3_codes", [P, N], U32)
-        w3_planes = sb("w3_planes", [P, N], U8)
-        nc.vector.tensor_copy(
-            w3_grouped[:].rearrange("p (c i j) -> p c j i", i=4, j=PACK),
-            w3_raw[:].rearrange("p j (c i) -> p c j i", i=4),
-        )
-        nc.vector.quantize_mx(out=w3_codes[:].bitcast(FP8X4), scales=w3_planes[:], in_=w3_grouped[:])
 
         for f, (j0, w) in enumerate(LAST_CHUNKS):
             c = j0 // CHUNKS[0][1]

@@ -2,6 +2,7 @@ import math
 from contextlib import ExitStack
 
 import concourse.mybir as mybir
+from concourse.masks import make_identity
 
 K, T, S, N, H = 1024, 2048, 512, 256, 512
 FLOPS = 2 * (2 * K * H * S + H * N * S)
@@ -19,7 +20,9 @@ ALU = mybir.AluOpType
 P = 128
 PACK = 4
 PASSES = K // (P * PACK)
-BANK_COLS = 128
+HALVES = 2
+HALF = H // HALVES
+TILES = S // P
 CHUNKS = [(0, 256), (256, 256)]
 LAST_CHUNKS = [(0, 256), (256, 128), (384, 128)]
 
@@ -41,35 +44,31 @@ def tile_picked_ylensg_fe_p_kernel(
         scale_table = sb("scale_table", [P, T], U8)
         x_codes = [sb(f"x_codes{o}", [P, S], U32) for o in range(PASSES)]
         x_planes = sb("x_planes", [P, S], U8)
+        identity = sb("identity", [P, P], F32)
+        make_identity(nc, identity[:])
 
         def load_x(o):
             nc.sync.dma_start(x_table[o][:], x_words[o].rearrange("p n t -> p (n t)").bitcast(I32))
 
-        def gather_x(o, j0, w):
-            picked = x_table[o][:].bitcast(U32).indirect(offs_sb[:, j0 // 16 : (j0 + w) // 16])
-            nc.vector.tensor_copy(x_codes[o][:, j0 : j0 + w], picked)
+        def gather_x(o):
+            nc.vector.tensor_copy(x_codes[o][:], x_table[o][:].bitcast(U32).indirect(offs_sb[:]))
 
-        def load_w(name, w, o, pieces):
-            raws = []
-            width = H // pieces
-            for h in range(pieces):
-                raw = sb(f"{name}_raw{o}_{h}", [P, PACK, width], F32)
-                rows = w[o * P * PACK : (o + 1) * P * PACK, h * width : (h + 1) * width]
-                nc.sync.dma_start(raw[:], rows.rearrange("(p j) c -> p j c", j=PACK))
-                raws.append(raw)
-            return raws
+        def load_rows(name, rows):
+            tile = sb(name, [P, PACK, rows.shape[1]], F32)
+            nc.sync.dma_start(tile[:], rows.rearrange("(p j) c -> p j c", j=PACK))
+            return tile
 
-        def quantise_w(name, raws, o):
-            grouped = sb(f"{name}_grouped{o}", [P, PACK * H], BF16)
-            view = grouped[:].rearrange("p (t a i j) -> p a t j i", t=PACK, i=4, j=PACK)
-            span = P // 4 // len(raws)
-            for h, raw in enumerate(raws):
-                nc.vector.tensor_copy(
-                    view[:, h * span : (h + 1) * span, :, :, :],
-                    raw[:].rearrange("p j (a t i) -> p a t j i", t=PACK, i=4),
-                )
-            codes = sb(f"{name}_codes{o}", [P, H], U32)
-            planes = sb(f"{name}_planes{o}", [P, H], U8)
+        def quantise(name, raw, on_scalar=False):
+            width = raw.shape[2]
+            grouped = sb(f"{name}_grouped", [P, PACK * width], BF16)
+            to = grouped[:].rearrange("p (c i j) -> p c j i", i=4, j=PACK)
+            fro = raw[:].rearrange("p j (c i) -> p c j i", i=4)
+            if on_scalar:
+                nc.scalar.copy(to, fro)
+            else:
+                nc.vector.tensor_copy(to, fro)
+            codes = sb(f"{name}_codes", [P, width], U32)
+            planes = sb(f"{name}_planes", [P, width], U8)
             nc.vector.quantize_mx(out=codes[:].bitcast(FP8X4), scales=planes[:], in_=grouped[:])
             return codes, planes
 
@@ -81,134 +80,138 @@ def tile_picked_ylensg_fe_p_kernel(
                 scale_table[32 * q : 32 * q + 4 * PASSES, :].bitcast(I32),
                 x_scales[:, 4 * q : 4 * q + 4, :].bitcast(I32),
             )
-        w1_raw = [load_w("w1", w1, 0, 1), load_w("w1", w1, 1, 1)]
         load_x(1)
-        w2_raw = [load_w("w2", w2, 0, 1), load_w("w2", w2, 1, 2)]
+        raw = {}
+        for h in range(HALVES):
+            for name, w in (("w1", w1), ("w2", w2)):
+                for o in range(PASSES):
+                    rows = w[o * P * PACK : (o + 1) * P * PACK, h * HALF : (h + 1) * HALF]
+                    raw[name, h, o] = load_rows(f"{name}_raw{h}{o}", rows)
         nc.sync.dma_start(src_sb[:], src)
+        ell_sb = load_rows("ell_sb", ell)
+        w3_raw = load_rows("w3_raw", w3)
+        unit_sb = sb("unit_sb", [P, PACK], F32)
+        nc.sync.dma_start(unit_sb[:], unit.rearrange("(p t) o -> p (t o)", t=PACK))
+        flx_sb = load_rows("flx_sb", flx)
 
-        def load_rows(queue, name, rows):
-            tile = sb(name, [P, PACK, rows.shape[1]], F32)
-            dealt = rows.rearrange("(a t i) c -> i a t c", t=PACK, i=4)
-            for i in range(4):
-                queue.dma_start(tile[i:P:4, :, :], dealt[i])
-            return tile
-
-        w3_raw = load_rows(nc.sync, "w3_raw", w3)
-        ell_sb = load_rows(nc.sync, "ell_sb", ell)
-        with nc.allow_non_contiguous_dma(reason="one value for each row"):
-            unit_sb = load_rows(nc.sync, "unit_sb", unit)
-        flx_sb = load_rows(nc.sync, "flx_sb", flx)
-
-        gather_x(0, 0, S)
+        gather_x(0)
         nc.vector.tensor_copy(x_planes[:], scale_table[:].indirect(offs_sb[:]))
-        w1_q = [quantise_w("w1", w1_raw[o], o) for o in range(PASSES)]
-        for j0, w in CHUNKS:
-            gather_x(1, j0, w)
+        gather_x(1)
 
-        def product(bank, wq, t, o, cols, start, stop):
-            codes, planes = wq[o]
-            m_cols = slice(t * P, (t + 1) * P)
-            nc.tensor.matmul_mx(
-                out=bank,
-                lhsT=codes[:, m_cols].bitcast(FP8X4),
-                lhsT_scale=planes[:, m_cols],
-                rhs=x_codes[o][:, cols].bitcast(FP8X4),
-                rhs_scale=x_planes[4 * o :, cols],
-                start=start,
-                stop=stop,
+        def products(name, h, first_bank):
+            banks = [
+                psum.tile([P, 2, HALF], F32, name=f"{name}_sum{h}{g}", tag=f"bank{first_bank + g}") for g in range(2)
+            ]
+            for o in range(PASSES):
+                codes, planes = quantise(f"{name}{h}{o}", raw[name, h, o])
+                for jt in range(TILES):
+                    cols = slice(jt * P, (jt + 1) * P)
+                    nc.tensor.matmul_mx(
+                        out=banks[jt // 2][:, jt % 2, :],
+                        lhsT=x_codes[o][:, cols].bitcast(FP8X4),
+                        lhsT_scale=x_planes[4 * o :, cols],
+                        rhs=codes[:].bitcast(FP8X4),
+                        rhs_scale=planes[:],
+                        start=o == 0 and jt % 2 == 0,
+                        stop=o == PASSES - 1 and jt % 2 == 1,
+                    )
+            return [bank[:].rearrange("p u (m t) -> p u t m", t=PACK) for bank in banks]
+
+        M = HALF // PACK
+        red = sb("red", [P, TILES, PACK, P], F32)
+        b_sq = sb("b_sq", [P, TILES, PACK, P], F32)
+        less = sb("less", [P, TILES, PACK, P], F32)
+        offset = sb("offset", [P, P], F32)
+        nc.gpsimd.memset(offset[:], 1.25)
+        for h in range(HALVES):
+            sig, tk, ts = (sb(f"{n}{h}", [P, TILES, PACK, M], F32) for n in ("sig", "tk", "ts"))
+            part = slice(h * M, (h + 1) * M)
+            kp = products("w1", h, 4 * h)
+            for g in range(2):
+                nc.scalar.activation(
+                    sig[:, 2 * g : 2 * g + 2], kp[g], ACT.Sigmoid, bias=-math.log(7.0 / 3.0), scale=2.0
+                )
+            for g in range(2):
+                nc.scalar.activation(tk[:, 2 * g : 2 * g + 2], kp[g], ACT.Tanh)
+            sh = products("w2", h, 4 * h + 2)
+            for g in range(2):
+                two = slice(2 * g, 2 * g + 2)
+                nc.scalar.activation(ts[:, two], sh[g], ACT.Tanh)
+                nc.vector.scalar_tensor_tensor(
+                    red[:, two, :, part].rearrange("p u t m -> p (u t) m"),
+                    sig[:, two].rearrange("p u t m -> p (u t) m"), 0.75,
+                    ts[:, two].rearrange("p u t m -> p (u t) m"), ALU.add, ALU.mult,
+                )
+            nc.scalar.activation(b_sq[:, :, :, part], tk[:], ACT.Square, bias=-2.5)
+            nc.vector.scalar_tensor_tensor(
+                less[:, :, :, part].rearrange("p u t m -> p (u t) m"),
+                ts[:].rearrange("p u t m -> p (u t) m"), -0.5625,
+                ts[:].rearrange("p u t m -> p (u t) m"), ALU.mult, ALU.mult,
             )
 
-        def chunk_tiles(name):
-            return [sb(f"{name}{c}", [P, PACK, w], F32) for c, (j0, w) in enumerate(CHUNKS)]
-
-        sig, tk, ts, g_sq, red, num = (chunk_tiles(n) for n in ("sig", "tk", "ts", "g_sq", "red", "num"))
-        paired, pair, den2, den, sgn, root = (chunk_tiles(n) for n in ("paired", "pair", "den2", "den", "sgn", "root"))
-        a_sq, inv, flux, signed = tk, root, num, num
-
-        kp_banks = {}
-        for c, (j0, w) in enumerate(CHUNKS):
-            for u in range(2):
-                kp_banks[c, u] = psum.tile([P, 2, w], F32, name=f"kp{c}{u}", tag=f"left{2 * c + u}")
-        for o in range(PASSES):
-            for c, (j0, w) in enumerate(CHUNKS):
+        def turn(name, terms, first_bank):
+            banks = []
+            for jt in range(TILES):
+                bank = psum.tile([P, PACK, P], F32, name=f"{name}{jt}", tag=f"bank{first_bank + jt}")
                 for t in range(PACK):
-                    product(
-                        kp_banks[c, t // 2][:, t % 2, :], w1_q, t, o, slice(j0, j0 + w),
-                        o == 0 and t % 2 == 0, o == PASSES - 1 and t % 2 == 1,
-                    )
-        for c in range(len(CHUNKS)):
-            for u in range(2):
-                nc.scalar.activation(
-                    sig[c][:, 2 * u : 2 * u + 2, :], kp_banks[c, u][:], ACT.Sigmoid, bias=-math.log(7.0 / 3.0), scale=2.0
-                )
-        for c in range(len(CHUNKS)):
-            for u in range(2):
-                nc.scalar.activation(tk[c][:, 2 * u : 2 * u + 2, :], kp_banks[c, u][:], ACT.Tanh)
+                    for n, term in enumerate(terms):
+                        nc.tensor.matmul(
+                            bank[:, t, :], term(jt, t), identity[:], start=n == 0, stop=n == len(terms) - 1, is_transpose=True
+                        )
+                banks.append(bank)
+            return banks
 
-        w2_q = [quantise_w("w2", w2_raw[o], o) for o in range(PASSES)]
-        n_banks = S // BANK_COLS
-        sh_banks = [psum.tile([P, PACK, BANK_COLS], F32, name=f"sh{b}", tag=f"right{b}") for b in range(n_banks)]
-        for o in range(PASSES):
-            for b in range(n_banks):
-                for t in range(PACK):
-                    product(
-                        sh_banks[b][:, t, :], w2_q, t, o, slice(b * BANK_COLS, (b + 1) * BANK_COLS),
-                        o == 0 and t == 0, o == PASSES - 1 and t == PACK - 1,
-                    )
-
-        w3_grouped = sb("w3_grouped", [P, N * PACK], BF16)
-        w3_codes = sb("w3_codes", [P, N], U32)
-        w3_planes = sb("w3_planes", [P, N], U8)
-        nc.vector.tensor_copy(
-            w3_grouped[:].rearrange("p (c i j) -> p c j i", i=4, j=PACK),
-            w3_raw[:].rearrange("p j (c i) -> p c j i", i=4),
+        num, paired, pair, den, sgn, root = (
+            sb(n, [P, PACK, S], F32) for n in ("num", "paired", "pair", "den", "sgn", "root")
         )
-        nc.vector.quantize_mx(out=w3_codes[:].bitcast(FP8X4), scales=w3_planes[:], in_=w3_grouped[:])
-
-        for c, (j0, w) in enumerate(CHUNKS):
-            for b in range(j0 // BANK_COLS, (j0 + w) // BANK_COLS):
-                part = slice(b * BANK_COLS - j0, (b + 1) * BANK_COLS - j0)
-                nc.scalar.activation(ts[c][:, :, part], sh_banks[b][:], ACT.Tanh)
-            nc.vector.scalar_tensor_tensor(red[c][:], sig[c][:], 0.75, ts[c][:], ALU.add, ALU.mult)
-        for c, (j0, w) in enumerate(CHUNKS):
-            cols = slice(j0, j0 + w)
+        signed = paired
+        red_t = turn("red_t", [lambda jt, t: red[:, jt, t, :]], 0)
+        for jt in range(TILES):
+            cols = slice(jt * P, (jt + 1) * P)
+            nc.vector.scalar_tensor_tensor(num[:, :, cols], red_t[jt][:], 2.0 / 7.0, ell_sb[:, :, cols], ALU.mult, ALU.add)
+        w3_codes, w3_planes = quantise("w3", w3_raw, True)
+        den2_t = turn(
+            "den2_t", [lambda jt, t: offset[:], lambda jt, t: b_sq[:, jt, t, :], lambda jt, t: less[:, jt, t, :]], 4
+        )
+        for t in range(PACK):
+            nc.vector.scalar_tensor_tensor(
+                num[:, t, :], num[:, t, :], unit_sb[:, t : t + 1], flx_sb[:, t, :], ALU.mult, ALU.mult
+            )
+        for j0, w in CHUNKS:
             for t in range(PACK):
                 nc.scalar.activation(
-                    paired[c][:, t, :], ell_sb[:, t, :].indirect(src_sb[:, j0 // 16 : (j0 + w) // 16]), ACT.Copy
+                    paired[:, t, j0 : j0 + w], ell_sb[:, t, :].indirect(src_sb[:, j0 // 16 : (j0 + w) // 16]), ACT.Copy
                 )
-            nc.vector.scalar_tensor_tensor(num[c][:], red[c][:], 2.0 / 7.0, ell_sb[:, :, cols], ALU.mult, ALU.add)
+            for jt in range(j0 // P, (j0 + w) // P):
+                cols = slice(jt * P, (jt + 1) * P)
+                nc.vector.scalar_tensor_tensor(pair[:, :, cols], red_t[jt][:], 2.0 / 7.0, paired[:, :, cols], ALU.mult, ALU.mult)
+            for jt in range(j0 // P, (j0 + w) // P):
+                cols = slice(jt * P, (jt + 1) * P)
+                nc.vector.scalar_tensor_tensor(den[:, :, cols], pair[:, :, cols], 1.0, den2_t[jt][:], ALU.add, ALU.mult)
         for c, (j0, w) in enumerate(CHUNKS):
             cols = slice(j0, j0 + w)
-            nc.vector.scalar_tensor_tensor(pair[c][:], red[c][:], 2.0 / 7.0, paired[c][:], ALU.mult, ALU.mult)
-            for t in range(PACK):
-                nc.vector.scalar_tensor_tensor(
-                    flux[c][:, t, :], num[c][:, t, :], unit_sb[:, t, :], flx_sb[:, t, cols], ALU.mult, ALU.mult
-                )
-        for c, (j0, w) in enumerate(CHUNKS):
-            nc.scalar.activation(a_sq[c][:], tk[c][:], ACT.Square, bias=1.0, scale=-0.4)
-            nc.scalar.activation(g_sq[c][:], ts[c][:], ACT.Square, scale=0.3)
-            nc.vector.scalar_tensor_tensor(den2[c][:], a_sq[c][:], 0.2, g_sq[c][:], ALU.add, ALU.subtract)
-            nc.vector.scalar_tensor_tensor(den[c][:], pair[c][:], 1.0, den2[c][:], ALU.add, ALU.mult)
-        for c, (j0, w) in enumerate(CHUNKS):
-            nc.scalar.activation(sgn[c][:], pair[c][:], ACT.Sign, bias=1.0)
-            nc.vector.tensor_tensor(signed[c][:], flux[c][:], sgn[c][:], ALU.mult)
+            if c < 2:
+                nc.scalar.activation(sgn[:, :, cols], pair[:, :, cols], ACT.Sign, bias=1.0)
+                nc.vector.tensor_tensor(signed[:, :, cols], num[:, :, cols], sgn[:, :, cols], ALU.mult)
+            else:
+                nc.vector.tensor_scalar(sgn[:, :, cols], pair[:, :, cols], -1.0, 0.5, ALU.is_ge, ALU.subtract)
+                nc.vector.scalar_tensor_tensor(signed[:, :, cols], sgn[:, :, cols], 2.0, num[:, :, cols], ALU.mult, ALU.mult)
 
         for f, (j0, w) in enumerate(LAST_CHUNKS):
-            c = j0 // CHUNKS[0][1]
-            part = slice(j0 - CHUNKS[c][0], j0 - CHUNKS[c][0] + w)
-            nc.scalar.activation(root[c][:, :, part], den[c][:, :, part], ACT.Abs_reciprocal_sqrt)
-            nc.scalar.activation(inv[c][:, :, part], root[c][:, :, part], ACT.Square)
+            cols = slice(j0, j0 + w)
+            nc.scalar.activation(root[:, :, cols], den[:, :, cols], ACT.Abs_reciprocal_sqrt)
+            nc.scalar.activation(root[:, :, cols], root[:, :, cols], ACT.Square, scale=2.5)
             hid = sb(f"hid{f}", [P, w * PACK], BF16)
             nc.vector.tensor_tensor(
                 hid[:].rearrange("p (c i t) -> p c t i", i=4, t=PACK),
-                signed[c][:, :, part].rearrange("p t (c i) -> p c t i", i=4),
-                inv[c][:, :, part].rearrange("p t (c i) -> p c t i", i=4),
+                signed[:, :, cols].rearrange("p t (c i) -> p c t i", i=4),
+                root[:, :, cols].rearrange("p t (c i) -> p c t i", i=4),
                 ALU.mult,
             )
             hid_codes = sb(f"hid_codes{f}", [P, w], U32)
             hid_planes = sb(f"hid_planes{f}", [P, w], U8)
             nc.vector.quantize_mx(out=hid_codes[:].bitcast(FP8X4), scales=hid_planes[:], in_=hid[:])
-            bins = psum.tile([P, N // P, w], F32, name=f"bins{f}", tag=f"left{f}")
+            bins = psum.tile([P, N // P, w], F32, name=f"bins{f}", tag=f"bank{f}")
             for mt in range(N // P):
                 m_cols = slice(mt * P, (mt + 1) * P)
                 nc.tensor.matmul_mx(

@@ -50,68 +50,77 @@ def tile_picked_ylensg_fe_p_kernel(
         def load_x(o):
             nc.sync.dma_start(x_table[o][:], x_words[o].rearrange("p n t -> p (n t)").bitcast(I32))
 
-        def gather_x(o):
-            nc.vector.tensor_copy(x_codes[o][:], x_table[o][:].bitcast(U32).indirect(offs_sb[:]))
+        def gather_x(o, j0, w):
+            picked = x_table[o][:].bitcast(U32).indirect(offs_sb[:, j0 // 16 : (j0 + w) // 16])
+            nc.vector.tensor_copy(x_codes[o][:, j0 : j0 + w], picked)
 
         def load_rows(name, rows):
             tile = sb(name, [P, PACK, rows.shape[1]], F32)
             nc.sync.dma_start(tile[:], rows.rearrange("(p j) c -> p j c", j=PACK))
             return tile
 
-        def quantise(name, raw, on_scalar=False):
-            width = raw.shape[2]
-            grouped = sb(f"{name}_grouped", [P, PACK * width], BF16)
-            to = grouped[:].rearrange("p (c i j) -> p c j i", i=4, j=PACK)
-            fro = raw[:].rearrange("p j (c i) -> p c j i", i=4)
-            if on_scalar:
-                nc.scalar.copy(to, fro)
-            else:
+        def quantise(name, raws):
+            width = raws[0].shape[2]
+            grouped = sb(f"{name}_grouped", [P, len(raws), PACK * width], BF16)
+            for n, rows in enumerate(raws):
+                to = grouped[:, n, :].rearrange("p (c i j) -> p c j i", i=4, j=PACK)
+                fro = rows[:].rearrange("p j (c i) -> p c j i", i=4)
                 nc.vector.tensor_copy(to, fro)
-            codes = sb(f"{name}_codes", [P, width], U32)
-            planes = sb(f"{name}_planes", [P, width], U8)
-            nc.vector.quantize_mx(out=codes[:].bitcast(FP8X4), scales=planes[:], in_=grouped[:])
-            return codes, planes
+            codes = sb(f"{name}_codes", [P, len(raws), width], U32)
+            planes = sb(f"{name}_planes", [P, len(raws), width], U8)
+            nc.vector.quantize_mx(
+                out=codes[:].rearrange("p n c -> p (n c)").bitcast(FP8X4),
+                scales=planes[:].rearrange("p n c -> p (n c)"),
+                in_=grouped[:].rearrange("p n c -> p (n c)"),
+            )
+            return [(codes[:, n, :], planes[:, n, :]) for n in range(len(raws))]
 
         nc.vector.memset(scale_table[:].bitcast(I32), 0)
         nc.sync.dma_start(offs_sb[:], offs)
-        load_x(0)
+        raw = {}
+
+        def load_half(name, w, h):
+            for o in range(PASSES):
+                rows = w[o * P * PACK : (o + 1) * P * PACK, h * HALF : (h + 1) * HALF]
+                raw[name, h, o] = load_rows(f"{name}_raw{h}{o}", rows)
+
+        load_half("w1", w1, 0)
         for q in range(4):
             nc.sync.dma_start(
                 scale_table[32 * q : 32 * q + 4 * PASSES, :].bitcast(I32),
                 x_scales[:, 4 * q : 4 * q + 4, :].bitcast(I32),
             )
+        load_x(0)
         load_x(1)
-        raw = {}
-        for h in range(HALVES):
-            for name, w in (("w1", w1), ("w2", w2)):
-                for o in range(PASSES):
-                    rows = w[o * P * PACK : (o + 1) * P * PACK, h * HALF : (h + 1) * HALF]
-                    raw[name, h, o] = load_rows(f"{name}_raw{h}{o}", rows)
+        load_half("w2", w2, 0)
+        load_half("w1", w1, 1)
+        load_half("w2", w2, 1)
         nc.sync.dma_start(src_sb[:], src)
         ell_sb = load_rows("ell_sb", ell)
+        flx_sb = load_rows("flx_sb", flx)
         w3_raw = load_rows("w3_raw", w3)
         unit_sb = sb("unit_sb", [P, PACK], F32)
         nc.sync.dma_start(unit_sb[:], unit.rearrange("(p t) o -> p (t o)", t=PACK))
-        flx_sb = load_rows("flx_sb", flx)
 
-        gather_x(0)
         nc.vector.tensor_copy(x_planes[:], scale_table[:].indirect(offs_sb[:]))
-        gather_x(1)
+        gather_x(0, 0, S)
+        for j0, w in CHUNKS:
+            gather_x(1, j0, w)
 
         def products(name, h, first_bank):
             banks = [
                 psum.tile([P, 2, HALF], F32, name=f"{name}_sum{h}{g}", tag=f"bank{first_bank + g}") for g in range(2)
             ]
             for o in range(PASSES):
-                codes, planes = quantise(f"{name}{h}{o}", raw[name, h, o])
+                codes, planes = quantise(f"{name}{h}{o}", [raw[name, h, o]])[0]
                 for jt in range(TILES):
                     cols = slice(jt * P, (jt + 1) * P)
                     nc.tensor.matmul_mx(
                         out=banks[jt // 2][:, jt % 2, :],
                         lhsT=x_codes[o][:, cols].bitcast(FP8X4),
                         lhsT_scale=x_planes[4 * o :, cols],
-                        rhs=codes[:].bitcast(FP8X4),
-                        rhs_scale=planes[:],
+                        rhs=codes.bitcast(FP8X4),
+                        rhs_scale=planes,
                         start=o == 0 and jt % 2 == 0,
                         stop=o == PASSES - 1 and jt % 2 == 1,
                     )
@@ -123,30 +132,40 @@ def tile_picked_ylensg_fe_p_kernel(
         less = sb("less", [P, TILES, PACK, P], F32)
         offset = sb("offset", [P, P], F32)
         nc.gpsimd.memset(offset[:], 1.25)
+        kp, sh = [], []
         for h in range(HALVES):
-            sig, tk, ts = (sb(f"{n}{h}", [P, TILES, PACK, M], F32) for n in ("sig", "tk", "ts"))
-            part = slice(h * M, (h + 1) * M)
-            kp = products("w1", h, 4 * h)
+            kp.append(products("w1", h, 4 * h))
+            sh.append(products("w2", h, 4 * h + 2))
+        sig, tk, ts = (
+            [sb(f"{n}{h}", [P, TILES, PACK, M], F32) for h in range(HALVES)] for n in ("sig", "tk", "ts")
+        )
+
+        def merged(view):
+            return view.rearrange("p u t m -> p (u t) m")
+
+        def half(tile, h):
+            return tile[:, :, :, h * M : (h + 1) * M]
+
+        for h in range(HALVES):
             for g in range(2):
                 nc.scalar.activation(
-                    sig[:, 2 * g : 2 * g + 2], kp[g], ACT.Sigmoid, bias=-math.log(7.0 / 3.0), scale=2.0
+                    sig[h][:, 2 * g : 2 * g + 2], kp[h][g], ACT.Sigmoid, bias=-math.log(7.0 / 3.0), scale=2.0
                 )
-            for g in range(2):
-                nc.scalar.activation(tk[:, 2 * g : 2 * g + 2], kp[g], ACT.Tanh)
-            sh = products("w2", h, 4 * h + 2)
             for g in range(2):
                 two = slice(2 * g, 2 * g + 2)
-                nc.scalar.activation(ts[:, two], sh[g], ACT.Tanh)
+                nc.scalar.activation(ts[h][:, two], sh[h][g], ACT.Tanh)
                 nc.vector.scalar_tensor_tensor(
-                    red[:, two, :, part].rearrange("p u t m -> p (u t) m"),
-                    sig[:, two].rearrange("p u t m -> p (u t) m"), 0.75,
-                    ts[:, two].rearrange("p u t m -> p (u t) m"), ALU.add, ALU.mult,
+                    merged(half(red, h)[:, two]), merged(sig[h][:, two]), 0.75, merged(ts[h][:, two]), ALU.add, ALU.mult
                 )
-            nc.scalar.activation(b_sq[:, :, :, part], tk[:], ACT.Square, bias=-2.5)
+
+        def convergence_square(h):
+            for g in range(2):
+                nc.scalar.activation(tk[h][:, 2 * g : 2 * g + 2], kp[h][g], ACT.Tanh)
+            nc.scalar.activation(half(b_sq, h), tk[h][:], ACT.Square, bias=-2.5)
+
+        def shear_square(h):
             nc.vector.scalar_tensor_tensor(
-                less[:, :, :, part].rearrange("p u t m -> p (u t) m"),
-                ts[:].rearrange("p u t m -> p (u t) m"), -0.5625,
-                ts[:].rearrange("p u t m -> p (u t) m"), ALU.mult, ALU.mult,
+                merged(half(less, h)), merged(ts[h][:]), -0.5625, merged(ts[h][:]), ALU.mult, ALU.mult
             )
 
         def turn(name, terms, first_bank):
@@ -165,37 +184,51 @@ def tile_picked_ylensg_fe_p_kernel(
             sb(n, [P, PACK, S], F32) for n in ("num", "paired", "pair", "den", "sgn", "root")
         )
         signed = paired
-        red_t = turn("red_t", [lambda jt, t: red[:, jt, t, :]], 0)
-        for jt in range(TILES):
-            cols = slice(jt * P, (jt + 1) * P)
-            nc.vector.scalar_tensor_tensor(num[:, :, cols], red_t[jt][:], 2.0 / 7.0, ell_sb[:, :, cols], ALU.mult, ALU.add)
-        w3_codes, w3_planes = quantise("w3", w3_raw, True)
-        den2_t = turn(
-            "den2_t", [lambda jt, t: offset[:], lambda jt, t: b_sq[:, jt, t, :], lambda jt, t: less[:, jt, t, :]], 4
-        )
-        for t in range(PACK):
-            nc.vector.scalar_tensor_tensor(
-                num[:, t, :], num[:, t, :], unit_sb[:, t : t + 1], flx_sb[:, t, :], ALU.mult, ALU.mult
-            )
-        for j0, w in CHUNKS:
+        def look_up(c):
+            j0, w = CHUNKS[c]
             for t in range(PACK):
                 nc.scalar.activation(
                     paired[:, t, j0 : j0 + w], ell_sb[:, t, :].indirect(src_sb[:, j0 // 16 : (j0 + w) // 16]), ACT.Copy
                 )
-            for jt in range(j0 // P, (j0 + w) // P):
-                cols = slice(jt * P, (jt + 1) * P)
+
+        def tiles_of(c):
+            j0, w = CHUNKS[c]
+            return [(jt, slice(jt * P, (jt + 1) * P)) for jt in range(j0 // P, (j0 + w) // P)]
+
+        def pair_step(c):
+            for jt, cols in tiles_of(c):
                 nc.vector.scalar_tensor_tensor(pair[:, :, cols], red_t[jt][:], 2.0 / 7.0, paired[:, :, cols], ALU.mult, ALU.mult)
-            for jt in range(j0 // P, (j0 + w) // P):
-                cols = slice(jt * P, (jt + 1) * P)
+
+        def den_step(c):
+            for jt, cols in tiles_of(c):
                 nc.vector.scalar_tensor_tensor(den[:, :, cols], pair[:, :, cols], 1.0, den2_t[jt][:], ALU.add, ALU.mult)
-        for c, (j0, w) in enumerate(CHUNKS):
+
+        convergence_square(0)
+        shear_square(0)
+        red_t = turn("red_t", [lambda jt, t: red[:, jt, t, :]], 0)
+        for jt in range(TILES):
+            cols = slice(jt * P, (jt + 1) * P)
+            nc.vector.scalar_tensor_tensor(num[:, :, cols], red_t[jt][:], 2.0 / 7.0, ell_sb[:, :, cols], ALU.mult, ALU.add)
+            nc.gpsimd.tensor_tensor(num[:, :, cols], num[:, :, cols], flx_sb[:, :, cols], ALU.mult)
+        look_up(0)
+        convergence_square(1)
+        shear_square(1)
+        den2_t = turn(
+            "den2_t", [lambda jt, t: offset[:], lambda jt, t: b_sq[:, jt, t, :], lambda jt, t: less[:, jt, t, :]], 4
+        )
+        pair_step(0)
+        look_up(1)
+        den_step(0)
+        pair_step(1)
+        den_step(1)
+        w3_codes, w3_planes = quantise("w3", [w3_raw])[0]
+        for j0, w in CHUNKS:
             cols = slice(j0, j0 + w)
-            if c < 2:
-                nc.scalar.activation(sgn[:, :, cols], pair[:, :, cols], ACT.Sign, bias=1.0)
-                nc.vector.tensor_tensor(signed[:, :, cols], num[:, :, cols], sgn[:, :, cols], ALU.mult)
-            else:
-                nc.vector.tensor_scalar(sgn[:, :, cols], pair[:, :, cols], -1.0, 0.5, ALU.is_ge, ALU.subtract)
-                nc.vector.scalar_tensor_tensor(signed[:, :, cols], sgn[:, :, cols], 2.0, num[:, :, cols], ALU.mult, ALU.mult)
+            nc.scalar.activation(sgn[:, :, cols], pair[:, :, cols], ACT.Sign, bias=1.0)
+            for t in range(PACK):
+                nc.vector.scalar_tensor_tensor(
+                    signed[:, t, cols], num[:, t, cols], unit_sb[:, t : t + 1], sgn[:, t, cols], ALU.mult, ALU.mult
+                )
 
         for f, (j0, w) in enumerate(LAST_CHUNKS):
             cols = slice(j0, j0 + w)

import math
from contextlib import ExitStack

import concourse.mybir as mybir
from concourse.masks import make_identity

K, T, S, N, H = 1024, 2048, 512, 256, 512
FLOPS = 2 * (2 * K * H * S + H * N * S)

F32 = mybir.dt.float32
BF16 = mybir.dt.bfloat16
I32 = mybir.dt.int32
U32 = mybir.dt.uint32
U16 = mybir.dt.uint16
U8 = mybir.dt.uint8
FP8X4 = mybir.dt.float8_e4m3fn_x4
ACT = mybir.ActivationFunctionType
ALU = mybir.AluOpType

P = 128
PACK = 4
PASSES = K // (P * PACK)
HALVES = 2
HALF = H // HALVES
TILES = S // P
CHUNKS = [(0, 256), (256, 256)]
LAST_CHUNKS = [(0, 256), (256, 128), (384, 128)]


def tile_picked_ylensg_fe_p_kernel(
    tc, x_words, x_scales, w1, w2, ell, flx, unit, w3, offs, src, out
):
    nc = tc.nc
    with ExitStack() as ctx:
        keep = ctx.enter_context(tc.tile_pool(name="keep", bufs=1))
        psum = ctx.enter_context(tc.psum_pool(name="psum", bufs=1))

        def sb(name, shape, dtype):
            return keep.tile(shape, dtype, name=name, align_bytes=64)

        offs_sb = keep.tile([P, S // 16], U16, name="offs_sb")
        src_sb = keep.tile([P, S // 16], U16, name="src_sb")
        x_table = [sb(f"x_table{o}", [P, T], I32) for o in range(PASSES)]
        scale_table = sb("scale_table", [P, T], U8)
        x_codes = [sb(f"x_codes{o}", [P, S], U32) for o in range(PASSES)]
        x_planes = sb("x_planes", [P, S], U8)
        identity = sb("identity", [P, P], F32)
        make_identity(nc, identity[:])

        def load_x(o):
            nc.sync.dma_start(x_table[o][:], x_words[o].rearrange("p n t -> p (n t)").bitcast(I32))

        def gather_x(o, j0, w):
            picked = x_table[o][:].bitcast(U32).indirect(offs_sb[:, j0 // 16 : (j0 + w) // 16])
            nc.vector.tensor_copy(x_codes[o][:, j0 : j0 + w], picked)

        def load_rows(name, rows):
            tile = sb(name, [P, PACK, rows.shape[1]], F32)
            nc.sync.dma_start(tile[:], rows.rearrange("(p j) c -> p j c", j=PACK))
            return tile

        def quantise(name, raws):
            width = raws[0].shape[2]
            grouped = sb(f"{name}_grouped", [P, len(raws), PACK * width], BF16)
            for n, rows in enumerate(raws):
                to = grouped[:, n, :].rearrange("p (c i j) -> p c j i", i=4, j=PACK)
                fro = rows[:].rearrange("p j (c i) -> p c j i", i=4)
                nc.vector.tensor_copy(to, fro)
            codes = sb(f"{name}_codes", [P, len(raws), width], U32)
            planes = sb(f"{name}_planes", [P, len(raws), width], U8)
            nc.vector.quantize_mx(
                out=codes[:].rearrange("p n c -> p (n c)").bitcast(FP8X4),
                scales=planes[:].rearrange("p n c -> p (n c)"),
                in_=grouped[:].rearrange("p n c -> p (n c)"),
            )
            return [(codes[:, n, :], planes[:, n, :]) for n in range(len(raws))]

        nc.vector.memset(scale_table[:].bitcast(I32), 0)
        nc.sync.dma_start(offs_sb[:], offs)
        raw = {}

        def load_half(name, w, h):
            for o in range(PASSES):
                rows = w[o * P * PACK : (o + 1) * P * PACK, h * HALF : (h + 1) * HALF]
                raw[name, h, o] = load_rows(f"{name}_raw{h}{o}", rows)

        load_half("w1", w1, 0)
        for q in range(4):
            nc.sync.dma_start(
                scale_table[32 * q : 32 * q + 4 * PASSES, :].bitcast(I32),
                x_scales[:, 4 * q : 4 * q + 4, :].bitcast(I32),
            )
        load_x(0)
        load_x(1)
        load_half("w2", w2, 0)
        load_half("w1", w1, 1)
        load_half("w2", w2, 1)
        nc.sync.dma_start(src_sb[:], src)
        ell_sb = load_rows("ell_sb", ell)
        flx_sb = load_rows("flx_sb", flx)
        w3_raw = load_rows("w3_raw", w3)
        unit_sb = sb("unit_sb", [P, PACK], F32)
        nc.sync.dma_start(unit_sb[:], unit.rearrange("(p t) o -> p (t o)", t=PACK))

        nc.vector.tensor_copy(x_planes[:], scale_table[:].indirect(offs_sb[:]))
        gather_x(0, 0, S)
        for j0, w in CHUNKS:
            gather_x(1, j0, w)

        def products(name, h, first_bank):
            banks = [
                psum.tile([P, 2, HALF], F32, name=f"{name}_sum{h}{g}", tag=f"bank{first_bank + g}") for g in range(2)
            ]
            for o in range(PASSES):
                codes, planes = quantise(f"{name}{h}{o}", [raw[name, h, o]])[0]
                for jt in range(TILES):
                    cols = slice(jt * P, (jt + 1) * P)
                    nc.tensor.matmul_mx(
                        out=banks[jt // 2][:, jt % 2, :],
                        lhsT=x_codes[o][:, cols].bitcast(FP8X4),
                        lhsT_scale=x_planes[4 * o :, cols],
                        rhs=codes.bitcast(FP8X4),
                        rhs_scale=planes,
                        start=o == 0 and jt % 2 == 0,
                        stop=o == PASSES - 1 and jt % 2 == 1,
                    )
            return [bank[:].rearrange("p u (m t) -> p u t m", t=PACK) for bank in banks]

        M = HALF // PACK
        red = sb("red", [P, TILES, PACK, P], F32)
        b_sq = sb("b_sq", [P, TILES, PACK, P], F32)
        less = sb("less", [P, TILES, PACK, P], F32)
        offset = sb("offset", [P, P], F32)
        nc.gpsimd.memset(offset[:], 1.25)
        kp, sh = [], []
        for h in range(HALVES):
            kp.append(products("w1", h, 4 * h))
            sh.append(products("w2", h, 4 * h + 2))
        sig, tk, ts = (
            [sb(f"{n}{h}", [P, TILES, PACK, M], F32) for h in range(HALVES)] for n in ("sig", "tk", "ts")
        )

        def merged(view):
            return view.rearrange("p u t m -> p (u t) m")

        def half(tile, h):
            return tile[:, :, :, h * M : (h + 1) * M]

        for h in range(HALVES):
            for g in range(2):
                nc.scalar.activation(
                    sig[h][:, 2 * g : 2 * g + 2], kp[h][g], ACT.Sigmoid, bias=-math.log(7.0 / 3.0), scale=2.0
                )
            for g in range(2):
                two = slice(2 * g, 2 * g + 2)
                nc.scalar.activation(ts[h][:, two], sh[h][g], ACT.Tanh)
                nc.vector.scalar_tensor_tensor(
                    merged(half(red, h)[:, two]), merged(sig[h][:, two]), 0.75, merged(ts[h][:, two]), ALU.add, ALU.mult
                )

        def convergence_square(h):
            for g in range(2):
                nc.scalar.activation(tk[h][:, 2 * g : 2 * g + 2], kp[h][g], ACT.Tanh)
            nc.scalar.activation(half(b_sq, h), tk[h][:], ACT.Square, bias=-2.5)

        def shear_square(h):
            nc.vector.scalar_tensor_tensor(
                merged(half(less, h)), merged(ts[h][:]), -0.5625, merged(ts[h][:]), ALU.mult, ALU.mult
            )

        def turn(name, terms, first_bank):
            banks = []
            for jt in range(TILES):
                bank = psum.tile([P, PACK, P], F32, name=f"{name}{jt}", tag=f"bank{first_bank + jt}")
                for t in range(PACK):
                    for n, term in enumerate(terms):
                        nc.tensor.matmul(
                            bank[:, t, :], term(jt, t), identity[:], start=n == 0, stop=n == len(terms) - 1, is_transpose=True
                        )
                banks.append(bank)
            return banks

        num, paired, pair, den, sgn, root = (
            sb(n, [P, PACK, S], F32) for n in ("num", "paired", "pair", "den", "sgn", "root")
        )
        signed = paired
        def look_up(c):
            j0, w = CHUNKS[c]
            for t in range(PACK):
                nc.scalar.activation(
                    paired[:, t, j0 : j0 + w], ell_sb[:, t, :].indirect(src_sb[:, j0 // 16 : (j0 + w) // 16]), ACT.Copy
                )

        def tiles_of(c):
            j0, w = CHUNKS[c]
            return [(jt, slice(jt * P, (jt + 1) * P)) for jt in range(j0 // P, (j0 + w) // P)]

        def pair_step(c):
            for jt, cols in tiles_of(c):
                nc.vector.scalar_tensor_tensor(pair[:, :, cols], red_t[jt][:], 2.0 / 7.0, paired[:, :, cols], ALU.mult, ALU.mult)

        def den_step(c):
            for jt, cols in tiles_of(c):
                nc.vector.scalar_tensor_tensor(den[:, :, cols], pair[:, :, cols], 1.0, den2_t[jt][:], ALU.add, ALU.mult)

        convergence_square(0)
        shear_square(0)
        red_t = turn("red_t", [lambda jt, t: red[:, jt, t, :]], 0)
        for jt in range(TILES):
            cols = slice(jt * P, (jt + 1) * P)
            nc.vector.scalar_tensor_tensor(num[:, :, cols], red_t[jt][:], 2.0 / 7.0, ell_sb[:, :, cols], ALU.mult, ALU.add)
            nc.gpsimd.tensor_tensor(num[:, :, cols], num[:, :, cols], flx_sb[:, :, cols], ALU.mult)
        look_up(0)
        convergence_square(1)
        shear_square(1)
        den2_t = turn(
            "den2_t", [lambda jt, t: offset[:], lambda jt, t: b_sq[:, jt, t, :], lambda jt, t: less[:, jt, t, :]], 4
        )
        pair_step(0)
        look_up(1)
        den_step(0)
        pair_step(1)
        den_step(1)
        w3_codes, w3_planes = quantise("w3", [w3_raw])[0]
        for j0, w in CHUNKS:
            cols = slice(j0, j0 + w)
            nc.scalar.activation(sgn[:, :, cols], pair[:, :, cols], ACT.Sign, bias=1.0)
            for t in range(PACK):
                nc.vector.scalar_tensor_tensor(
                    signed[:, t, cols], num[:, t, cols], unit_sb[:, t : t + 1], sgn[:, t, cols], ALU.mult, ALU.mult
                )

        for f, (j0, w) in enumerate(LAST_CHUNKS):
            cols = slice(j0, j0 + w)
            nc.scalar.activation(root[:, :, cols], den[:, :, cols], ACT.Abs_reciprocal_sqrt)
            nc.scalar.activation(root[:, :, cols], root[:, :, cols], ACT.Square, scale=2.5)
            hid = sb(f"hid{f}", [P, w * PACK], BF16)
            nc.vector.tensor_tensor(
                hid[:].rearrange("p (c i t) -> p c t i", i=4, t=PACK),
                signed[:, :, cols].rearrange("p t (c i) -> p c t i", i=4),
                root[:, :, cols].rearrange("p t (c i) -> p c t i", i=4),
                ALU.mult,
            )
            hid_codes = sb(f"hid_codes{f}", [P, w], U32)
            hid_planes = sb(f"hid_planes{f}", [P, w], U8)
            nc.vector.quantize_mx(out=hid_codes[:].bitcast(FP8X4), scales=hid_planes[:], in_=hid[:])
            bins = psum.tile([P, N // P, w], F32, name=f"bins{f}", tag=f"bank{f}")
            for mt in range(N // P):
                m_cols = slice(mt * P, (mt + 1) * P)
                nc.tensor.matmul_mx(
                    out=bins[:, mt, :],
                    lhsT=w3_codes[:, m_cols].bitcast(FP8X4),
                    lhsT_scale=w3_planes[:, m_cols],
                    rhs=hid_codes[:].bitcast(FP8X4),
                    rhs_scale=hid_planes[:],
                    start=True,
                    stop=True,
                )
            result = sb(f"result{f}", [P, N // P, w], F32)
            nc.scalar.copy(result[:], bins[:])
            nc.sync.dma_start(out[:, j0 : j0 + w].rearrange("(m p) c -> p m c", p=P), result[:])
